import numpy as np
import ml_dtypes


def mxq(x, axis, fmt="e4m3"):
    dtype, down = {"e4m3": (ml_dtypes.float8_e4m3fn, 7), "e5m2": (ml_dtypes.float8_e5m2, 14)}[fmt]
    v = np.moveaxis(np.asarray(x, np.float32).astype(ml_dtypes.bfloat16).astype(np.float64), axis, -1)
    blocks = v.reshape(v.shape[:-1] + (-1, 32))
    amax = np.abs(blocks).max(-1, keepdims=True)
    byte = np.maximum(np.where(amax > 0, np.frexp(amax)[1] - 1 + 127, 0) - down, 1)
    scale = np.exp2(byte - 127.0)
    codes = (blocks / scale).astype(np.float32).astype(dtype).astype(np.float64)
    return np.moveaxis((codes * scale).reshape(v.shape), -1, axis)


WIDE = False


def mx_kscale(k):
    if not WIDE:
        return np.ones(k)
    levels = np.array([10, -10, 5, -5, 0])
    if k % 512:
        return np.exp2(np.random.permutation(np.resize(levels, k // 32))).repeat(32)
    a = np.empty((k // 512, 16))
    for p in range(k // 512):
        a[p, :8] = np.random.permutation(np.resize(levels, 8))
        for g in range(8):
            far = levels[np.abs(levels - a[p, g]) >= 10]
            a[p, g + 8] = far[np.random.randint(len(far))]
    return np.exp2(a.ravel()).repeat(32)


def f64(x):
    return np.asarray(x).astype(np.float64)


def striped(idx):
    return np.tile(np.asarray(idx).reshape(-1, 16).T, (8, 1)).astype(np.uint16)


def unstriped(offs):
    return offs[:16].T.reshape(-1).astype(np.int64)


B, N, T, D, DV, NQ = 2, 512, 2048, 512, 256, 128


def setup_inputs():
    n = np.random.standard_normal
    seg = T // B
    idx = np.concatenate([b * seg + np.random.permutation(seg)[:N] for b in range(B)])
    s = mx_kscale(D)[:, None]
    u = np.ones(T)
    u[idx] = mx_kscale(B * N)
    r = np.random.uniform(0.5, 2.0, T)
    k = n((D, T)) / s
    v = n((DV, T)) / (u * r)
    return {
        "qT": (n((B, D, NQ)) * s * (0.70 / np.sqrt(D))).astype(np.float32),
        "kT": k.astype(np.float32),
        "vT": v.astype(np.float32),
        "vs": np.tile(u * r, (128, 1)).astype(np.float32),
        "kb": np.tile(n(T), (128, 1)).astype(np.float32),
        "og": n((B, NQ, DV)).astype(np.float32),
        "offs": striped(idx),
    }


def reference(qT, kT, vT, vs, kb, og, offs):
    idx = unstriped(offs)
    k = f64(kT)
    v = f64(vT)
    pick = lambda x: x[:, idx].reshape(x.shape[0], B, N).transpose(1, 0, 2)
    q = f64(qT)
    score = mxq(q, 1, "e4m3").transpose(0, 2, 1) @ mxq(pick(k), 1, "e4m3")
    score = score + pick(f64(kb))[:, :1, :]
    p = score / (1.0 + np.exp(-score))
    w = p * pick(f64(vs))[:, :1, :]
    y = mxq(w, 2, "e4m3") @ mxq(pick(v).transpose(0, 2, 1), 1, "e4m3")
    y = y / 16.0
    y = y / (1.0 + np.exp(-f64(og)))
    return y

@@ -1,0 +1,245 @@
+from contextlib import ExitStack
+
+import concourse.mybir as mybir
+from concourse.masks import make_identity
+
+B, N, T, D, DV, NQ = 2, 512, 2048, 512, 256, 128
+SEG = T // B
+P = 128
+PACK = 4
+HALF = SEG // 2
+LIST = N // 16
+
+FLOPS = 2 * B * N * NQ * (D + DV)
+BYTES = 4 * (B * D * NQ + D * T + DV * T + 2 * T + 2 * B * NQ * DV) + 2 * B * N
+
+F32 = mybir.dt.float32
+BF16 = mybir.dt.bfloat16
+U32 = mybir.dt.uint32
+U16 = mybir.dt.uint16
+U8 = mybir.dt.uint8
+FP8X4 = mybir.dt.float8_e4m3fn_x4
+ACT = mybir.ActivationFunctionType
+ALU = mybir.AluOpType
+
+
+def tile_attend_hstu_seg_kernel(tc, qT, kT, vT, vs, kb, og, offs, out):
+    nc = tc.nc
+    with ExitStack() as ctx:
+        hold = ctx.enter_context(tc.tile_pool(name="hold", bufs=1))
+        psum = ctx.enter_context(tc.psum_pool(name="psum", bufs=2))
+
+        offsets = hold.tile([P, B * LIST], U16, name="offsets")
+        nc.sync.dma_start(offsets[:], offs)
+
+        def listed(b):
+            return offsets[:, b * LIST : (b + 1) * LIST]
+
+        warm = hold.tile([P, 8], F32, name="warm")
+        warmed = hold.tile([P, 8], F32, name="warmed")
+        nc.gpsimd.memset(warm[:], 0.0)
+        nc.scalar.activation(warmed[:], warm[:], ACT.Silu)
+
+        kb_pool = hold.tile([P, T], F32, name="kb_pool")
+        vs_pool = hold.tile([P, T], F32, name="vs_pool")
+        for b in range(B):
+            cols = slice(b * SEG, (b + 1) * SEG)
+            nc.vector.memset(kb_pool[:, cols], 0.0)
+            nc.vector.memset(vs_pool[:, cols], 0.0)
+
+        ident = hold.tile([P, P], F32, name="ident")
+        make_identity(nc, ident[:])
+
+        k_rows = kT.rearrange("(p j) n -> p j n", j=PACK)
+        v_rows = vT.rearrange("(p j) n -> p j n", j=2)
+        raw = {}
+
+        def load(key, src, start, width):
+            t = hold.tile([P, 2, width], F32, name="raw_%s_%d" % (key, start))
+            nc.sync.dma_start(t[:], src[:, :, start : start + width])
+            raw[(key, start)] = t
+
+        k_pairs = [k_rows[:, 2 * u : 2 * u + 2, :] for u in range(2)]
+        def load_rows(b):
+            cols = slice(b * SEG, (b + 1) * SEG)
+            nc.sync.dma_start(kb_pool[0:1, cols], kb[0:1, cols])
+            nc.sync.dma_start(vs_pool[0:1, cols], vs[0:1, cols])
+
+        def load_halves(key, src, b):
+            for h in range(2):
+                load(key, src, b * SEG + h * HALF, HALF)
+
+        for b in range(B):
+            load_halves("k0", k_pairs[0], b)
+            if b == 0:
+                load_rows(0)
+            else:
+                q_raw = hold.tile([P, B, PACK, NQ], F32, name="q_raw")
+                nc.sync.dma_start(q_raw[:], qT.rearrange("b (p j) q -> p b j q", j=PACK))
+            load_halves("k1", k_pairs[1], b)
+            if b == 0:
+                load_rows(1)
+        load_halves("v", v_rows, 0)
+        og_raw = hold.tile([P, B, DV], F32, name="og_raw")
+        nc.sync.dma_start(og_raw[:], og.rearrange("b q e -> q b e"))
+        load_halves("v", v_rows, 1)
+
+        packed = {}
+        for key in ("k0", "k1", "v"):
+            packed[key] = hold.tile([P, 2 * T], BF16, name="packed_" + key)
+
+        def pack(engine, key, start, width):
+            dst = packed[key][:, 2 * start : 2 * (start + width)].rearrange("p (n j) -> p n j", j=2)
+            src = raw[(key, start)][:].rearrange("p j n -> p n j")
+            if engine == "s":
+                nc.scalar.activation(dst, src, ACT.Copy)
+            else:
+                nc.vector.tensor_copy(dst, src)
+
+        def gather_words(dst, key, b):
+            words = packed[key][:].bitcast(U32)
+            nc.vector.tensor_copy(dst, words[:, 0 : (b + 1) * SEG].indirect(listed(b)))
+
+        cols = {}
+
+        def gather_column(kind, pool, b):
+            row = hold.tile([P, N], F32, name="row_%s_%d" % (kind, b))
+            nc.vector.tensor_copy(row[:], pool[:, 0 : (b + 1) * SEG].indirect(listed(b)))
+            turned = psum.tile([P, PACK, P], F32, name="turned_%s_%d" % (kind, b), tag="turned")
+            for t in range(PACK):
+                nc.tensor.transpose(turned[:, t, :], row[:, t:N:PACK], ident[:])
+            col = hold.tile([P, PACK, 1], F32, name="col_%s_%d" % (kind, b))
+            nc.vector.tensor_copy(col[:], turned[:, :, 0:1])
+            cols[(kind, b)] = col
+
+        k_codes, k_scales = {}, {}
+
+        def keys(b):
+            got = hold.tile([P, 2, 2 * N], BF16, name="k_got_%d" % b)
+            for u in range(2):
+                gather_words(got[:, u, :].bitcast(U32), "k%d" % u, b)
+            grouped = hold.tile([P, PACK * N], BF16, name="k_grouped_%d" % b, align_bytes=64)
+            nc.vector.tensor_copy(
+                grouped[:].bitcast(F32).rearrange("p (t m u) -> p m t u", t=PACK, u=2),
+                got[:].bitcast(F32).rearrange("p u (m t) -> p m t u", t=PACK),
+            )
+            codes = hold.tile([P, N], U32, name="k_codes_%d" % b, align_bytes=64)
+            scales = hold.tile([P, N], U8, name="k_scales_%d" % b, align_bytes=64)
+            nc.vector.quantize_mx(out=codes[:].bitcast(FP8X4), scales=scales[:], in_=grouped[:])
+            k_codes[b], k_scales[b] = codes, scales
+
+        q_codes = hold.tile([P, B * NQ], U32, name="q_codes", align_bytes=64)
+        q_scales = hold.tile([P, B * NQ], U8, name="q_scales", align_bytes=64)
+
+        def queries():
+            grouped = hold.tile([P, B, NQ, PACK], BF16, name="q_grouped", align_bytes=64)
+            for b in range(B):
+                nc.gpsimd.tensor_scalar(
+                    grouped[:, b, :, :], q_raw[:, b, :, :].rearrange("p j q -> p q j"), 1.0, 0.0, ALU.mult, ALU.add
+                )
+            nc.vector.quantize_mx(
+                out=q_codes[:].bitcast(FP8X4), scales=q_scales[:], in_=grouped[:].rearrange("p b q j -> p (b q j)")
+            )
+
+        scores, w_codes, w_scales = {}, {}, {}
+
+        def score(b):
+            scores[b] = psum.tile([P, PACK, NQ], F32, name="score_%d" % b, tag="score")
+            qc = slice(b * NQ, (b + 1) * NQ)
+            for t in range(PACK):
+                kc = slice(t * P, (t + 1) * P)
+                nc.tensor.matmul_mx(
+                    out=scores[b][:, t, :],
+                    lhsT=k_codes[b][:, kc].bitcast(FP8X4),
+                    lhsT_scale=k_scales[b][:, kc],
+                    rhs=q_codes[:, qc].bitcast(FP8X4),
+                    rhs_scale=q_scales[:, qc],
+                    start=True,
+                    stop=True,
+                )
+
+        def weigh(b):
+            p = hold.tile([P, PACK, NQ], F32, name="p_%d" % b)
+            for t in range(PACK):
+                nc.scalar.activation(p[:, t, :], scores[b][:, t, :], ACT.Silu, bias=cols[("kb", b)][:, t, :])
+            w = hold.tile([P, NQ, PACK], BF16, name="w_%d" % b, align_bytes=64)
+            nc.vector.tensor_tensor(
+                w[:],
+                p[:].rearrange("p t q -> p q t"),
+                cols[("vs", b)][:].rearrange("p t o -> p o t").to_broadcast([P, NQ, PACK]),
+                ALU.mult,
+            )
+            codes = hold.tile([P, NQ], U32, name="w_codes_%d" % b, align_bytes=64)
+            scales = hold.tile([P, NQ], U8, name="w_scales_%d" % b, align_bytes=64)
+            nc.vector.quantize_mx(
+                out=codes[:].bitcast(FP8X4), scales=scales[:], in_=w[:].rearrange("p q t -> p (q t)")
+            )
+            w_codes[b], w_scales[b] = codes, scales
+
+        v_codes, v_scales = {}, {}
+
+        def values(b):
+            got = hold.tile([P, 2 * N], BF16, name="v_got_%d" % b)
+            gather_words(got[:].bitcast(U32), "v", b)
+            turned = psum.tile([P, PACK, P], F32, name="v_turned_%d" % b, tag="v_turned")
+            words = got[:].bitcast(F32)
+            for t in range(PACK):
+                nc.tensor.transpose(turned[:, t, :], words[:, t:N:PACK], ident[:])
+            grouped = hold.tile([P, DV, PACK], BF16, name="v_grouped_%d" % b, align_bytes=64)
+            nc.scalar.copy(grouped[:], turned[:].bitcast(BF16).rearrange("p t e -> p e t"))
+            codes = hold.tile([P, DV], U32, name="v_codes_%d" % b, align_bytes=64)
+            scales = hold.tile([P, DV], U8, name="v_scales_%d" % b, align_bytes=64)
+            nc.vector.quantize_mx(
+                out=codes[:].bitcast(FP8X4), scales=scales[:], in_=grouped[:].rearrange("p e t -> p (e t)")
+            )
+            v_codes[b], v_scales[b] = codes, scales
+
+        gate = hold.tile([P, B, DV], F32, name="gate")
+
+        def gates():
+            th = hold.tile([P, B, DV], F32, name="th")
+            nc.scalar.activation(th[:], og_raw[:], ACT.Tanh, scale=0.5)
+            nc.gpsimd.tensor_scalar(gate[:], th[:], 0.03125, 0.03125, ALU.mult, ALU.add)
+
+        def finish(b):
+            y = psum.tile([P, DV], F32, name="y_%d" % b, tag="y")
+            nc.tensor.matmul_mx(
+                out=y[:],
+                lhsT=w_codes[b][:].bitcast(FP8X4),
+                lhsT_scale=w_scales[b][:],
+                rhs=v_codes[b][:].bitcast(FP8X4),
+                rhs_scale=v_scales[b][:],
+                start=True,
+                stop=True,
+            )
+            res = hold.tile([P, DV], F32, name="res_%d" % b)
+            nc.vector.tensor_tensor(res[:], y[:], gate[:, b, :], ALU.mult)
+            nc.sync.dma_start(out[b], res[:])
+
+        def pack_both(key, b):
+            for h in range(2):
+                pack("s", key, b * SEG + h * HALF, HALF)
+
+        gather_column("kb", kb_pool, 0)
+        gather_column("vs", vs_pool, 0)
+        pack_both("k0", 0)
+        pack_both("k1", 0)
+        gather_column("kb", kb_pool, 1)
+        gather_column("vs", vs_pool, 1)
+        keys(0)
+        queries()
+        score(0)
+        pack_both("k0", 1)
+        weigh(0)
+        pack_both("k1", 1)
+        keys(1)
+        score(1)
+        pack_both("v", 0)
+        gates()
+        values(0)
+        weigh(1)
+        finish(0)
+        pack("s", "v", SEG, HALF)
+        pack("v", "v", SEG + HALF, HALF)
+        values(1)
+        finish(1)

@@ -35,63 +35,37 @@ def tile_attend_hstu_seg_kernel(tc, qT, kT, vT, vs, kb, og, offs, out):
         def listed(b):
             return offsets[:, b * LIST : (b + 1) * LIST]
 
-        warm = hold.tile([P, 8], F32, name="warm")
-        warmed = hold.tile([P, 8], F32, name="warmed")
-        nc.gpsimd.memset(warm[:], 0.0)
-        nc.scalar.activation(warmed[:], warm[:], ACT.Silu)
-
-        kb_pool = hold.tile([P, T], F32, name="kb_pool")
-        vs_pool = hold.tile([P, T], F32, name="vs_pool")
+        tokens = {}
         for b in range(B):
-            cols = slice(b * SEG, (b + 1) * SEG)
-            nc.vector.memset(kb_pool[:, cols], 0.0)
-            nc.vector.memset(vs_pool[:, cols], 0.0)
-
-        ident = hold.tile([P, P], F32, name="ident")
-        make_identity(nc, ident[:])
-
+            for kind in ("kb", "vs"):
+                tokens[(kind, b)] = hold.tile([P, (b + 1) * SEG], F32, name="%s_pool_%d" % (kind, b))
+        source = {"kb": kb, "vs": vs}
         k_rows = kT.rearrange("(p j) n -> p j n", j=PACK)
-        v_rows = vT.rearrange("(p j) n -> p j n", j=2)
-        raw = {}
+        pools = {"k0": k_rows[:, 0:2, :], "k1": k_rows[:, 2:4, :], "v": vT.rearrange("(p j) n -> p j n", j=2)}
+        raw, packed, cols = {}, {}, {}
+        got, grouped, codes, scales, banks, weights, gate = {}, {}, {}, {}, {}, {}, {}
 
-        def load(key, src, start, width):
-            t = hold.tile([P, 2, width], F32, name="raw_%s_%d" % (key, start))
-            nc.sync.dma_start(t[:], src[:, :, start : start + width])
-            raw[(key, start)] = t
+        def zero(engine, kind, b):
+            engine.memset(tokens[(kind, b)][:], 0.0)
 
-        k_pairs = [k_rows[:, 2 * u : 2 * u + 2, :] for u in range(2)]
-        def load_rows(b):
-            cols = slice(b * SEG, (b + 1) * SEG)
-            nc.sync.dma_start(kb_pool[0:1, cols], kb[0:1, cols])
-            nc.sync.dma_start(vs_pool[0:1, cols], vs[0:1, cols])
+        def load_row(queue, kind, b):
+            s = slice(b * SEG, (b + 1) * SEG)
+            queue.dma_start(tokens[(kind, b)][0:1, s], source[kind][0:1, s])
 
-        def load_halves(key, src, b):
-            for h in range(2):
-                load(key, src, b * SEG + h * HALF, HALF)
+        def load(key, b, h):
+            start = b * SEG + h * HALF
+            t = hold.tile([P, 2, HALF], F32, name="raw_%s_%d_%d" % (key, b, h))
+            nc.sync.dma_start(t[:], pools[key][:, :, start : start + HALF])
+            raw[(key, b, h)] = t
 
-        for b in range(B):
-            load_halves("k0", k_pairs[0], b)
-            if b == 0:
-                load_rows(0)
-            else:
-                q_raw = hold.tile([P, B, PACK, NQ], F32, name="q_raw")
-                nc.sync.dma_start(q_raw[:], qT.rearrange("b (p j) q -> p b j q", j=PACK))
-            load_halves("k1", k_pairs[1], b)
-            if b == 0:
-                load_rows(1)
-        load_halves("v", v_rows, 0)
-        og_raw = hold.tile([P, B, DV], F32, name="og_raw")
-        nc.sync.dma_start(og_raw[:], og.rearrange("b q e -> q b e"))
-        load_halves("v", v_rows, 1)
-
-        packed = {}
         for key in ("k0", "k1", "v"):
             packed[key] = hold.tile([P, 2 * T], BF16, name="packed_" + key)
 
-        def pack(engine, key, start, width):
-            dst = packed[key][:, 2 * start : 2 * (start + width)].rearrange("p (n j) -> p n j", j=2)
-            src = raw[(key, start)][:].rearrange("p j n -> p n j")
-            if engine == "s":
+        def pack(engine, key, b, h):
+            start = b * SEG + h * HALF
+            dst = packed[key][:, 2 * start : 2 * (start + HALF)].rearrange("p (n j) -> p n j", j=2)
+            src = raw[(key, b, h)][:].rearrange("p j n -> p n j")
+            if engine == "S":
                 nc.scalar.activation(dst, src, ACT.Copy)
             else:
                 nc.vector.tensor_copy(dst, src)
@@ -100,146 +74,199 @@ def tile_attend_hstu_seg_kernel(tc, qT, kT, vT, vs, kb, og, offs, out):
             words = packed[key][:].bitcast(U32)
             nc.vector.tensor_copy(dst, words[:, 0 : (b + 1) * SEG].indirect(listed(b)))
 
-        cols = {}
-
-        def gather_column(kind, pool, b):
+        def gather_row(kind, b):
             row = hold.tile([P, N], F32, name="row_%s_%d" % (kind, b))
-            nc.vector.tensor_copy(row[:], pool[:, 0 : (b + 1) * SEG].indirect(listed(b)))
+            nc.vector.tensor_copy(row[:], tokens[(kind, b)][:].indirect(listed(b)))
+            got[(kind, b)] = row
+
+        def turn_row(kind, b):
             turned = psum.tile([P, PACK, P], F32, name="turned_%s_%d" % (kind, b), tag="turned")
             for t in range(PACK):
-                nc.tensor.transpose(turned[:, t, :], row[:, t:N:PACK], ident[:])
+                nc.tensor.transpose(turned[:, t, :], got[(kind, b)][:, t:N:PACK], ident[:])
+            banks[(kind, b)] = turned
+
+        def column(kind, b):
             col = hold.tile([P, PACK, 1], F32, name="col_%s_%d" % (kind, b))
-            nc.vector.tensor_copy(col[:], turned[:, :, 0:1])
+            nc.vector.tensor_copy(col[:], banks[(kind, b)][:, :, 0:1])
             cols[(kind, b)] = col
 
-        k_codes, k_scales = {}, {}
+        def gather_keys(b, u):
+            if u == 0:
+                got[("k", b)] = hold.tile([P, 2, 2 * N], BF16, name="k_got_%d" % b)
+            gather_words(got[("k", b)][:, u, :].bitcast(U32), "k%d" % u, b)
 
-        def keys(b):
-            got = hold.tile([P, 2, 2 * N], BF16, name="k_got_%d" % b)
-            for u in range(2):
-                gather_words(got[:, u, :].bitcast(U32), "k%d" % u, b)
-            grouped = hold.tile([P, PACK * N], BF16, name="k_grouped_%d" % b, align_bytes=64)
+        def group_keys(b):
+            t4 = hold.tile([P, PACK * N], BF16, name="k_grouped_%d" % b, align_bytes=64)
             nc.vector.tensor_copy(
-                grouped[:].bitcast(F32).rearrange("p (t m u) -> p m t u", t=PACK, u=2),
-                got[:].bitcast(F32).rearrange("p u (m t) -> p m t u", t=PACK),
+                t4[:].bitcast(F32).rearrange("p (t m u) -> p m t u", t=PACK, u=2),
+                got[("k", b)][:].bitcast(F32).rearrange("p u (m t) -> p m t u", t=PACK),
             )
-            codes = hold.tile([P, N], U32, name="k_codes_%d" % b, align_bytes=64)
-            scales = hold.tile([P, N], U8, name="k_scales_%d" % b, align_bytes=64)
-            nc.vector.quantize_mx(out=codes[:].bitcast(FP8X4), scales=scales[:], in_=grouped[:])
-            k_codes[b], k_scales[b] = codes, scales
+            grouped[("k", b)] = t4
 
-        q_codes = hold.tile([P, B * NQ], U32, name="q_codes", align_bytes=64)
-        q_scales = hold.tile([P, B * NQ], U8, name="q_scales", align_bytes=64)
+        def quantize(what, b, width):
+            c = hold.tile([P, width], U32, name="codes_%s_%d" % (what, b), align_bytes=64)
+            s = hold.tile([P, width], U8, name="scales_%s_%d" % (what, b), align_bytes=64)
+            nc.vector.quantize_mx(out=c[:].bitcast(FP8X4), scales=s[:], in_=grouped[(what, b)][:])
+            codes[(what, b)], scales[(what, b)] = c, s
 
-        def queries():
-            grouped = hold.tile([P, B, NQ, PACK], BF16, name="q_grouped", align_bytes=64)
+        def group_queries():
+            t4 = hold.tile([P, B * NQ * PACK], BF16, name="q_grouped", align_bytes=64)
+            view = t4[:].rearrange("p (b q j) -> p b q j", b=B, j=PACK)
             for b in range(B):
                 nc.gpsimd.tensor_scalar(
-                    grouped[:, b, :, :], q_raw[:, b, :, :].rearrange("p j q -> p q j"), 1.0, 0.0, ALU.mult, ALU.add
+                    view[:, b, :, :], q_raw[:, b, :, :].rearrange("p j q -> p q j"), 1.0, 0.0, ALU.mult, ALU.add
                 )
-            nc.vector.quantize_mx(
-                out=q_codes[:].bitcast(FP8X4), scales=q_scales[:], in_=grouped[:].rearrange("p b q j -> p (b q j)")
-            )
+            grouped[("q", 0)] = t4
 
-        scores, w_codes, w_scales = {}, {}, {}
+        def mx(bank, left, lc, right, rc):
+            nc.tensor.matmul_mx(
+                out=bank,
+                lhsT=codes[left][:, lc].bitcast(FP8X4),
+                lhsT_scale=scales[left][:, lc],
+                rhs=codes[right][:, rc].bitcast(FP8X4),
+                rhs_scale=scales[right][:, rc],
+                start=True,
+                stop=True,
+            )
 
         def score(b):
-            scores[b] = psum.tile([P, PACK, NQ], F32, name="score_%d" % b, tag="score")
-            qc = slice(b * NQ, (b + 1) * NQ)
+            bank = psum.tile([P, PACK, NQ], F32, name="score_%d" % b, tag="score")
             for t in range(PACK):
-                kc = slice(t * P, (t + 1) * P)
-                nc.tensor.matmul_mx(
-                    out=scores[b][:, t, :],
-                    lhsT=k_codes[b][:, kc].bitcast(FP8X4),
-                    lhsT_scale=k_scales[b][:, kc],
-                    rhs=q_codes[:, qc].bitcast(FP8X4),
-                    rhs_scale=q_scales[:, qc],
-                    start=True,
-                    stop=True,
-                )
+                mx(bank[:, t, :], ("k", b), slice(t * P, (t + 1) * P), ("q", 0), slice(b * NQ, (b + 1) * NQ))
+            banks[("s", b)] = bank
 
-        def weigh(b):
+        def silu(b):
             p = hold.tile([P, PACK, NQ], F32, name="p_%d" % b)
             for t in range(PACK):
-                nc.scalar.activation(p[:, t, :], scores[b][:, t, :], ACT.Silu, bias=cols[("kb", b)][:, t, :])
-            w = hold.tile([P, NQ, PACK], BF16, name="w_%d" % b, align_bytes=64)
+                nc.scalar.activation(p[:, t, :], banks[("s", b)][:, t, :], ACT.Silu, bias=cols[("kb", b)][:, t, :])
+            weights[b] = p
+
+        def weigh(b):
+            t4 = hold.tile([P, NQ * PACK], BF16, name="w_%d" % b, align_bytes=64)
+            view = t4[:].rearrange("p (q t) -> p q t", t=PACK)
+            scale = cols[("vs", b)][:].rearrange("p t o -> p o t")
             nc.vector.tensor_tensor(
-                w[:],
-                p[:].rearrange("p t q -> p q t"),
-                cols[("vs", b)][:].rearrange("p t o -> p o t").to_broadcast([P, NQ, PACK]),
-                ALU.mult,
+                view, weights[b][:].rearrange("p t q -> p q t"), scale.to_broadcast([P, NQ, PACK]), ALU.mult
             )
-            codes = hold.tile([P, NQ], U32, name="w_codes_%d" % b, align_bytes=64)
-            scales = hold.tile([P, NQ], U8, name="w_scales_%d" % b, align_bytes=64)
-            nc.vector.quantize_mx(
-                out=codes[:].bitcast(FP8X4), scales=scales[:], in_=w[:].rearrange("p q t -> p (q t)")
-            )
-            w_codes[b], w_scales[b] = codes, scales
+            grouped[("w", b)] = t4
 
-        v_codes, v_scales = {}, {}
+        def gather_values(b):
+            got[("v", b)] = hold.tile([P, 2 * N], BF16, name="v_got_%d" % b)
+            gather_words(got[("v", b)][:].bitcast(U32), "v", b)
 
-        def values(b):
-            got = hold.tile([P, 2 * N], BF16, name="v_got_%d" % b)
-            gather_words(got[:].bitcast(U32), "v", b)
+        def turn_values(b):
             turned = psum.tile([P, PACK, P], F32, name="v_turned_%d" % b, tag="v_turned")
-            words = got[:].bitcast(F32)
+            words = got[("v", b)][:].bitcast(F32)
             for t in range(PACK):
                 nc.tensor.transpose(turned[:, t, :], words[:, t:N:PACK], ident[:])
-            grouped = hold.tile([P, DV, PACK], BF16, name="v_grouped_%d" % b, align_bytes=64)
-            nc.scalar.copy(grouped[:], turned[:].bitcast(BF16).rearrange("p t e -> p e t"))
-            codes = hold.tile([P, DV], U32, name="v_codes_%d" % b, align_bytes=64)
-            scales = hold.tile([P, DV], U8, name="v_scales_%d" % b, align_bytes=64)
-            nc.vector.quantize_mx(
-                out=codes[:].bitcast(FP8X4), scales=scales[:], in_=grouped[:].rearrange("p e t -> p (e t)")
-            )
-            v_codes[b], v_scales[b] = codes, scales
+            banks[("v", b)] = turned
 
-        gate = hold.tile([P, B, DV], F32, name="gate")
+        def group_values(b):
+            t4 = hold.tile([P, DV * PACK], BF16, name="v_grouped_%d" % b, align_bytes=64)
+            nc.scalar.copy(
+                t4[:].rearrange("p (e t) -> p e t", t=PACK), banks[("v", b)][:].bitcast(BF16).rearrange("p t e -> p e t")
+            )
+            grouped[("v", b)] = t4
 
         def gates():
             th = hold.tile([P, B, DV], F32, name="th")
             nc.scalar.activation(th[:], og_raw[:], ACT.Tanh, scale=0.5)
-            nc.gpsimd.tensor_scalar(gate[:], th[:], 0.03125, 0.03125, ALU.mult, ALU.add)
+            gate[0] = hold.tile([P, B, DV], F32, name="gate")
+            nc.gpsimd.tensor_scalar(gate[0][:], th[:], 0.03125, 0.03125, ALU.mult, ALU.add)
 
-        def finish(b):
+        def product(b):
             y = psum.tile([P, DV], F32, name="y_%d" % b, tag="y")
-            nc.tensor.matmul_mx(
-                out=y[:],
-                lhsT=w_codes[b][:].bitcast(FP8X4),
-                lhsT_scale=w_scales[b][:],
-                rhs=v_codes[b][:].bitcast(FP8X4),
-                rhs_scale=v_scales[b][:],
-                start=True,
-                stop=True,
-            )
+            mx(y[:], ("w", b), slice(0, NQ), ("v", b), slice(0, DV))
+            banks[("y", b)] = y
+
+        def store(b):
             res = hold.tile([P, DV], F32, name="res_%d" % b)
-            nc.vector.tensor_tensor(res[:], y[:], gate[:, b, :], ALU.mult)
+            nc.vector.tensor_tensor(res[:], banks[("y", b)][:], gate[0][:, b, :], ALU.mult)
             nc.sync.dma_start(out[b], res[:])
 
-        def pack_both(key, b):
-            for h in range(2):
-                pack("s", key, b * SEG + h * HALF, HALF)
+        warm = hold.tile([P, 8], F32, name="warm")
+        warmed = hold.tile([P, 8], F32, name="warmed")
+        zero(nc.gpsimd, "kb", 0)
+        nc.vector.memset(warm[:], 0.0)
+        nc.scalar.activation(warmed[:], warm[:], ACT.Silu)
+        zero(nc.vector, "vs", 0)
+        load("k0", 0, 0)
+        load_row(nc.sync, "kb", 0)
+        load_row(nc.sync, "vs", 0)
+        load("k0", 0, 1)
+        ident = hold.tile([P, P], F32, name="ident")
+        make_identity(nc, ident[:])
+        zero(nc.vector, "kb", 1)
+        zero(nc.vector, "vs", 1)
+        load("k1", 0, 0)
+        load("k1", 0, 1)
+        load_row(nc.sync, "kb", 1)
+        load_row(nc.sync, "vs", 1)
+        load("k0", 1, 0)
+        load("k0", 1, 1)
+        q_raw = hold.tile([P, B, PACK, NQ], F32, name="q_raw")
+        nc.sync.dma_start(q_raw[:], qT.rearrange("b (p j) q -> p b j q", j=PACK))
+        load("k1", 1, 0)
+        load("k1", 1, 1)
+        load("v", 0, 0)
+        load("v", 0, 1)
+        og_raw = hold.tile([P, B, DV], F32, name="og_raw")
+        nc.sync.dma_start(og_raw[:], og.rearrange("b q e -> q b e"))
+        load("v", 1, 0)
+        load("v", 1, 1)
 
-        gather_column("kb", kb_pool, 0)
-        gather_column("vs", vs_pool, 0)
-        pack_both("k0", 0)
-        pack_both("k1", 0)
-        gather_column("kb", kb_pool, 1)
-        gather_column("vs", vs_pool, 1)
-        keys(0)
-        queries()
+        pack("V", "k0", 0, 0)
+        gather_row("kb", 0)
+        turn_row("kb", 0)
+        pack("S", "k0", 0, 1)
+        gather_row("vs", 0)
+        turn_row("vs", 0)
+        pack("S", "k1", 0, 0)
+        gather_keys(0, 0)
+        column("kb", 0)
+        pack("S", "k1", 0, 1)
+        column("vs", 0)
+        gather_keys(0, 1)
+        pack("S", "k0", 1, 0)
+        gather_row("kb", 1)
+        turn_row("kb", 1)
+        pack("S", "k0", 1, 1)
+        group_queries()
+        group_keys(0)
+        pack("S", "k1", 1, 0)
+        gather_keys(1, 0)
+        quantize("k", 0, N)
+        quantize("q", 0, B * NQ)
         score(0)
-        pack_both("k0", 1)
+        pack("S", "k1", 1, 1)
+        gather_row("vs", 1)
+        turn_row("vs", 1)
+        column("kb", 1)
+        silu(0)
+        gather_keys(1, 1)
+        column("vs", 1)
         weigh(0)
-        pack_both("k1", 1)
-        keys(1)
-        score(1)
-        pack_both("v", 0)
+        pack("S", "v", 0, 0)
+        group_keys(1)
+        pack("S", "v", 0, 1)
+        quantize("w", 0, NQ)
+        gather_values(0)
+        turn_values(0)
         gates()
-        values(0)
+        pack("S", "v", 1, 0)
+        quantize("k", 1, N)
+        score(1)
+        group_values(0)
+        silu(1)
+        pack("V", "v", 1, 1)
+        gather_values(1)
+        turn_values(1)
+        quantize("v", 0, DV)
+        product(0)
         weigh(1)
-        finish(0)
-        pack("s", "v", SEG, HALF)
-        pack("v", "v", SEG + HALF, HALF)
-        values(1)
-        finish(1)
+        group_values(1)
+        quantize("w", 1, NQ)
+        store(0)
+        quantize("v", 1, DV)
+        product(1)
+        store(1)

@@ -36,9 +36,8 @@ def tile_attend_hstu_seg_kernel(tc, qT, kT, vT, vs, kb, og, offs, out):
             return offsets[:, b * LIST : (b + 1) * LIST]
 
         tokens = {}
-        for b in range(B):
-            for kind in ("kb", "vs"):
-                tokens[(kind, b)] = hold.tile([P, (b + 1) * SEG], F32, name="%s_pool_%d" % (kind, b))
+        for kind in ("kb", "vs"):
+            tokens[kind] = hold.tile([P, T], F32, name="%s_pool" % kind)
         source = {"kb": kb, "vs": vs}
         k_rows = kT.rearrange("(p j) n -> p j n", j=PACK)
         pools = {"k0": k_rows[:, 0:2, :], "k1": k_rows[:, 2:4, :], "v": vT.rearrange("(p j) n -> p j n", j=2)}
@@ -46,11 +45,10 @@ def tile_attend_hstu_seg_kernel(tc, qT, kT, vT, vs, kb, og, offs, out):
         got, grouped, codes, scales, banks, weights, gate = {}, {}, {}, {}, {}, {}, {}
 
         def zero(engine, kind, b):
-            engine.memset(tokens[(kind, b)][:], 0.0)
+            engine.memset(tokens[kind][:, b * SEG : (b + 1) * SEG], 0.0)
 
-        def load_row(queue, kind, b):
-            s = slice(b * SEG, (b + 1) * SEG)
-            queue.dma_start(tokens[(kind, b)][0:1, s], source[kind][0:1, s])
+        def load_row(kind):
+            nc.sync.dma_start(tokens[kind][0:1, :], source[kind][0:1, :])
 
         def load(key, b, h):
             start = b * SEG + h * HALF
@@ -59,11 +57,12 @@ def tile_attend_hstu_seg_kernel(tc, qT, kT, vT, vs, kb, og, offs, out):
             raw[(key, b, h)] = t
 
         for key in ("k0", "k1", "v"):
-            packed[key] = hold.tile([P, 2 * T], BF16, name="packed_" + key)
+            for b in range(B):
+                packed[(key, b)] = hold.tile([P, 2 * (b + 1) * SEG], BF16, name="packed_%s_%d" % (key, b))
 
         def pack(engine, key, b, h):
             start = b * SEG + h * HALF
-            dst = packed[key][:, 2 * start : 2 * (start + HALF)].rearrange("p (n j) -> p n j", j=2)
+            dst = packed[(key, b)][:, 2 * start : 2 * (start + HALF)].rearrange("p (n j) -> p n j", j=2)
             src = raw[(key, b, h)][:].rearrange("p j n -> p n j")
             if engine == "S":
                 nc.scalar.activation(dst, src, ACT.Copy)
@@ -71,18 +70,17 @@ def tile_attend_hstu_seg_kernel(tc, qT, kT, vT, vs, kb, og, offs, out):
                 nc.vector.tensor_copy(dst, src)
 
         def gather_words(dst, key, b):
-            words = packed[key][:].bitcast(U32)
-            nc.vector.tensor_copy(dst, words[:, 0 : (b + 1) * SEG].indirect(listed(b)))
+            nc.vector.tensor_copy(dst, packed[(key, b)][:].bitcast(U32).indirect(listed(b)))
 
-        def gather_row(kind, b):
-            row = hold.tile([P, N], F32, name="row_%s_%d" % (kind, b))
-            nc.vector.tensor_copy(row[:], tokens[(kind, b)][:].indirect(listed(b)))
-            got[(kind, b)] = row
+        def gather_row(kind):
+            row = hold.tile([P, B * N], F32, name="row_%s" % kind)
+            nc.vector.tensor_copy(row[:], tokens[kind][:].indirect(offsets[:]))
+            got[kind] = row
 
         def turn_row(kind, b):
             turned = psum.tile([P, PACK, P], F32, name="turned_%s_%d" % (kind, b), tag="turned")
             for t in range(PACK):
-                nc.tensor.transpose(turned[:, t, :], got[(kind, b)][:, t:N:PACK], ident[:])
+                nc.tensor.transpose(turned[:, t, :], got[kind][:, b * N + t : (b + 1) * N : PACK], ident[:])
             banks[(kind, b)] = turned
 
         def column(kind, b):
@@ -95,9 +93,10 @@ def tile_attend_hstu_seg_kernel(tc, qT, kT, vT, vs, kb, og, offs, out):
                 got[("k", b)] = hold.tile([P, 2, 2 * N], BF16, name="k_got_%d" % b)
             gather_words(got[("k", b)][:, u, :].bitcast(U32), "k%d" % u, b)
 
-        def group_keys(b):
+        def group_keys(engine, b):
             t4 = hold.tile([P, PACK * N], BF16, name="k_grouped_%d" % b, align_bytes=64)
-            nc.vector.tensor_copy(
+            copy = nc.scalar.copy if engine == "S" else nc.vector.tensor_copy
+            copy(
                 t4[:].bitcast(F32).rearrange("p (t m u) -> p m t u", t=PACK, u=2),
                 got[("k", b)][:].bitcast(F32).rearrange("p u (m t) -> p m t u", t=PACK),
             )
@@ -141,13 +140,12 @@ def tile_attend_hstu_seg_kernel(tc, qT, kT, vT, vs, kb, og, offs, out):
                 nc.scalar.activation(p[:, t, :], banks[("s", b)][:, t, :], ACT.Silu, bias=cols[("kb", b)][:, t, :])
             weights[b] = p
 
-        def weigh(b):
+        def weigh(engine, b):
             t4 = hold.tile([P, NQ * PACK], BF16, name="w_%d" % b, align_bytes=64)
             view = t4[:].rearrange("p (q t) -> p q t", t=PACK)
             scale = cols[("vs", b)][:].rearrange("p t o -> p o t")
-            nc.vector.tensor_tensor(
-                view, weights[b][:].rearrange("p t q -> p q t"), scale.to_broadcast([P, NQ, PACK]), ALU.mult
-            )
+            multiply = nc.gpsimd.tensor_tensor if engine == "G" else nc.vector.tensor_tensor
+            multiply(view, weights[b][:].rearrange("p t q -> p q t"), scale.to_broadcast([P, NQ, PACK]), ALU.mult)
             grouped[("w", b)] = t4
 
         def gather_values(b):
@@ -184,88 +182,86 @@ def tile_attend_hstu_seg_kernel(tc, qT, kT, vT, vs, kb, og, offs, out):
             nc.vector.tensor_tensor(res[:], banks[("y", b)][:], gate[0][:, b, :], ALU.mult)
             nc.sync.dma_start(out[b], res[:])
 
+        q_raw = hold.tile([P, B, PACK, NQ], F32, name="q_raw")
+        og_raw = hold.tile([P, B, DV], F32, name="og_raw")
         warm = hold.tile([P, 8], F32, name="warm")
         warmed = hold.tile([P, 8], F32, name="warmed")
         zero(nc.gpsimd, "kb", 0)
         nc.vector.memset(warm[:], 0.0)
         nc.scalar.activation(warmed[:], warm[:], ACT.Silu)
-        zero(nc.vector, "vs", 0)
+        zero(nc.vector, "kb", 1)
+        zero(nc.gpsimd, "vs", 0)
+        zero(nc.vector, "vs", 1)
         load("k0", 0, 0)
-        load_row(nc.sync, "kb", 0)
-        load_row(nc.sync, "vs", 0)
+        load_row("kb")
         load("k0", 0, 1)
+        load("k1", 0, 0)
+        load_row("vs")
+        load("k1", 0, 1)
         ident = hold.tile([P, P], F32, name="ident")
         make_identity(nc, ident[:])
-        zero(nc.vector, "kb", 1)
-        zero(nc.vector, "vs", 1)
-        load("k1", 0, 0)
-        load("k1", 0, 1)
-        load_row(nc.sync, "kb", 1)
-        load_row(nc.sync, "vs", 1)
+        for key in ("k0", "k1", "v"):
+            nc.gpsimd.memset(packed[(key, 1)][:, 0 : 2 * SEG].bitcast(F32), 0.0)
+        nc.sync.dma_start(q_raw[:], qT.rearrange("b (p j) q -> p b j q", j=PACK))
         load("k0", 1, 0)
         load("k0", 1, 1)
-        q_raw = hold.tile([P, B, PACK, NQ], F32, name="q_raw")
-        nc.sync.dma_start(q_raw[:], qT.rearrange("b (p j) q -> p b j q", j=PACK))
         load("k1", 1, 0)
         load("k1", 1, 1)
         load("v", 0, 0)
         load("v", 0, 1)
-        og_raw = hold.tile([P, B, DV], F32, name="og_raw")
         nc.sync.dma_start(og_raw[:], og.rearrange("b q e -> q b e"))
         load("v", 1, 0)
         load("v", 1, 1)
 
-        pack("V", "k0", 0, 0)
-        gather_row("kb", 0)
+        gather_row("kb")
         turn_row("kb", 0)
+        turn_row("kb", 1)
+        pack("S", "k0", 0, 0)
         pack("S", "k0", 0, 1)
-        gather_row("vs", 0)
+        gather_row("vs")
+        column("kb", 0)
+        column("kb", 1)
         turn_row("vs", 0)
+        turn_row("vs", 1)
         pack("S", "k1", 0, 0)
         gather_keys(0, 0)
-        column("kb", 0)
-        pack("S", "k1", 0, 1)
         column("vs", 0)
+        column("vs", 1)
+        pack("S", "k1", 0, 1)
         gather_keys(0, 1)
-        pack("S", "k0", 1, 0)
-        gather_row("kb", 1)
-        turn_row("kb", 1)
-        pack("S", "k0", 1, 1)
         group_queries()
-        group_keys(0)
-        pack("S", "k1", 1, 0)
-        gather_keys(1, 0)
-        quantize("k", 0, N)
+        group_keys("V", 0)
         quantize("q", 0, B * NQ)
+        pack("S", "k0", 1, 0)
+        quantize("k", 0, N)
         score(0)
+        pack("S", "k0", 1, 1)
+        gather_keys(1, 0)
+        pack("S", "k1", 1, 0)
         pack("S", "k1", 1, 1)
-        gather_row("vs", 1)
-        turn_row("vs", 1)
-        column("kb", 1)
         silu(0)
         gather_keys(1, 1)
-        column("vs", 1)
-        weigh(0)
+        weigh("V", 0)
         pack("S", "v", 0, 0)
-        group_keys(1)
-        pack("S", "v", 0, 1)
+        group_keys("V", 1)
         quantize("w", 0, NQ)
-        gather_values(0)
-        turn_values(0)
-        gates()
-        pack("S", "v", 1, 0)
+        pack("S", "v", 0, 1)
         quantize("k", 1, N)
         score(1)
-        group_values(0)
+        gather_values(0)
+        turn_values(0)
         silu(1)
+        gates()
+        pack("S", "v", 1, 0)
+        weigh("V", 1)
         pack("V", "v", 1, 1)
+        group_values(0)
         gather_values(1)
         turn_values(1)
+        quantize("w", 1, NQ)
         quantize("v", 0, DV)
         product(0)
-        weigh(1)
         group_values(1)
-        quantize("w", 1, NQ)
         store(0)
         quantize("v", 1, DV)
         product(1)

@@ -44,11 +44,12 @@ def tile_attend_hstu_seg_kernel(tc, qT, kT, vT, vs, kb, og, offs, out):
         raw, packed, cols = {}, {}, {}
         got, grouped, codes, scales, banks, weights, gate = {}, {}, {}, {}, {}, {}, {}
 
-        def zero(engine, kind, b):
-            engine.memset(tokens[kind][:, b * SEG : (b + 1) * SEG], 0.0)
+        def zero(kind, b):
+            nc.vector.memset(tokens[kind][:, b * SEG : (b + 1) * SEG], 0.0)
 
-        def load_row(kind):
-            nc.sync.dma_start(tokens[kind][0:1, :], source[kind][0:1, :])
+        def load_row(kind, b):
+            s = slice(b * SEG, (b + 1) * SEG)
+            nc.sync.dma_start(tokens[kind][0:1, s], source[kind][0:1, s])
 
         def load(key, b, h):
             start = b * SEG + h * HALF
@@ -57,12 +58,11 @@ def tile_attend_hstu_seg_kernel(tc, qT, kT, vT, vs, kb, og, offs, out):
             raw[(key, b, h)] = t
 
         for key in ("k0", "k1", "v"):
-            for b in range(B):
-                packed[(key, b)] = hold.tile([P, 2 * (b + 1) * SEG], BF16, name="packed_%s_%d" % (key, b))
+            packed[key] = hold.tile([P, 2 * T], BF16, name="packed_" + key)
 
         def pack(engine, key, b, h):
             start = b * SEG + h * HALF
-            dst = packed[(key, b)][:, 2 * start : 2 * (start + HALF)].rearrange("p (n j) -> p n j", j=2)
+            dst = packed[key][:, 2 * start : 2 * (start + HALF)].rearrange("p (n j) -> p n j", j=2)
             src = raw[(key, b, h)][:].rearrange("p j n -> p n j")
             if engine == "S":
                 nc.scalar.activation(dst, src, ACT.Copy)
@@ -70,17 +70,18 @@ def tile_attend_hstu_seg_kernel(tc, qT, kT, vT, vs, kb, og, offs, out):
                 nc.vector.tensor_copy(dst, src)
 
         def gather_words(dst, key, b):
-            nc.vector.tensor_copy(dst, packed[(key, b)][:].bitcast(U32).indirect(listed(b)))
+            words = packed[key][:].bitcast(U32)
+            nc.vector.tensor_copy(dst, words[:, 0 : (b + 1) * SEG].indirect(listed(b)))
 
-        def gather_row(kind):
-            row = hold.tile([P, B * N], F32, name="row_%s" % kind)
-            nc.vector.tensor_copy(row[:], tokens[kind][:].indirect(offsets[:]))
-            got[kind] = row
+        def gather_row(kind, b):
+            row = hold.tile([P, N], F32, name="row_%s_%d" % (kind, b))
+            nc.vector.tensor_copy(row[:], tokens[kind][:, 0 : (b + 1) * SEG].indirect(listed(b)))
+            got[(kind, b)] = row
 
         def turn_row(kind, b):
             turned = psum.tile([P, PACK, P], F32, name="turned_%s_%d" % (kind, b), tag="turned")
             for t in range(PACK):
-                nc.tensor.transpose(turned[:, t, :], got[kind][:, b * N + t : (b + 1) * N : PACK], ident[:])
+                nc.tensor.transpose(turned[:, t, :], got[(kind, b)][:, t:N:PACK], ident[:])
             banks[(kind, b)] = turned
 
         def column(kind, b):
@@ -186,25 +187,25 @@ def tile_attend_hstu_seg_kernel(tc, qT, kT, vT, vs, kb, og, offs, out):
         og_raw = hold.tile([P, B, DV], F32, name="og_raw")
         warm = hold.tile([P, 8], F32, name="warm")
         warmed = hold.tile([P, 8], F32, name="warmed")
-        zero(nc.gpsimd, "kb", 0)
-        nc.vector.memset(warm[:], 0.0)
+        nc.gpsimd.memset(warm[:], 0.0)
         nc.scalar.activation(warmed[:], warm[:], ACT.Silu)
-        zero(nc.vector, "kb", 1)
-        zero(nc.gpsimd, "vs", 0)
-        zero(nc.vector, "vs", 1)
-        load("k0", 0, 0)
-        load_row("kb")
-        load("k0", 0, 1)
-        load("k1", 0, 0)
-        load_row("vs")
-        load("k1", 0, 1)
         ident = hold.tile([P, P], F32, name="ident")
         make_identity(nc, ident[:])
-        for key in ("k0", "k1", "v"):
-            nc.gpsimd.memset(packed[(key, 1)][:, 0 : 2 * SEG].bitcast(F32), 0.0)
-        nc.sync.dma_start(q_raw[:], qT.rearrange("b (p j) q -> p b j q", j=PACK))
+        zero("kb", 0)
+        zero("vs", 0)
+        zero("kb", 1)
+        zero("vs", 1)
+        load("k0", 0, 0)
+        load_row("kb", 0)
+        load_row("vs", 0)
+        load("k0", 0, 1)
+        load("k1", 0, 0)
+        load_row("kb", 1)
+        load_row("vs", 1)
+        load("k1", 0, 1)
         load("k0", 1, 0)
         load("k0", 1, 1)
+        nc.sync.dma_start(q_raw[:], qT.rearrange("b (p j) q -> p b j q", j=PACK))
         load("k1", 1, 0)
         load("k1", 1, 1)
         load("v", 0, 0)
@@ -213,54 +214,56 @@ def tile_attend_hstu_seg_kernel(tc, qT, kT, vT, vs, kb, og, offs, out):
         load("v", 1, 0)
         load("v", 1, 1)
 
-        gather_row("kb")
-        turn_row("kb", 0)
-        turn_row("kb", 1)
         pack("S", "k0", 0, 0)
+        gather_row("kb", 0)
+        turn_row("kb", 0)
         pack("S", "k0", 0, 1)
-        gather_row("vs")
-        column("kb", 0)
-        column("kb", 1)
+        gather_row("vs", 0)
         turn_row("vs", 0)
-        turn_row("vs", 1)
         pack("S", "k1", 0, 0)
         gather_keys(0, 0)
-        column("vs", 0)
-        column("vs", 1)
+        column("kb", 0)
         pack("S", "k1", 0, 1)
+        column("vs", 0)
+        gather_row("kb", 1)
+        turn_row("kb", 1)
         gather_keys(0, 1)
-        group_queries()
-        group_keys("V", 0)
-        quantize("q", 0, B * NQ)
         pack("S", "k0", 1, 0)
-        quantize("k", 0, N)
-        score(0)
+        gather_row("vs", 1)
+        turn_row("vs", 1)
         pack("S", "k0", 1, 1)
+        column("kb", 1)
+        group_keys("V", 0)
+        group_queries()
         gather_keys(1, 0)
+        column("vs", 1)
         pack("S", "k1", 1, 0)
+        quantize("k", 0, N)
+        quantize("q", 0, B * NQ)
+        score(0)
         pack("S", "k1", 1, 1)
-        silu(0)
         gather_keys(1, 1)
-        weigh("V", 0)
         pack("S", "v", 0, 0)
+        silu(0)
         group_keys("V", 1)
-        quantize("w", 0, NQ)
         pack("S", "v", 0, 1)
+        gates()
         quantize("k", 1, N)
         score(1)
         gather_values(0)
         turn_values(0)
         silu(1)
-        gates()
         pack("S", "v", 1, 0)
-        weigh("V", 1)
         pack("V", "v", 1, 1)
+        weigh("V", 0)
+        quantize("w", 0, NQ)
         group_values(0)
         gather_values(1)
         turn_values(1)
-        quantize("w", 1, NQ)
+        weigh("V", 1)
         quantize("v", 0, DV)
         product(0)
+        quantize("w", 1, NQ)
         group_values(1)
         store(0)
         quantize("v", 1, DV)

@@ -4,9 +4,10 @@ import concourse.mybir as mybir
 from concourse.masks import make_identity
 
 B, N, T, D, DV, NQ = 2, 512, 2048, 512, 256, 128
-SEG = T // B
 P = 128
 PACK = 4
+PAIR = 2
+SEG = T // B
 HALF = SEG // 2
 LIST = N // 16
 
@@ -38,70 +39,60 @@ def tile_attend_hstu_seg_kernel(tc, qT, kT, vT, vs, kb, og, offs, out):
         tokens = {}
         for kind in ("kb", "vs"):
             tokens[kind] = hold.tile([P, T], F32, name="%s_pool" % kind)
-        source = {"kb": kb, "vs": vs}
-        k_rows = kT.rearrange("(p j) n -> p j n", j=PACK)
-        pools = {"k0": k_rows[:, 0:2, :], "k1": k_rows[:, 2:4, :], "v": vT.rearrange("(p j) n -> p j n", j=2)}
-        raw, packed, cols = {}, {}, {}
-        got, grouped, codes, scales, banks, weights, gate = {}, {}, {}, {}, {}, {}, {}
+        token_rows = {"kb": kb, "vs": vs}
 
-        def zero(kind, b):
+        k_rows = kT.rearrange("(p j) n -> p j n", j=PACK)
+        pair_rows = {
+            "k0": k_rows[:, 0:PAIR, :],
+            "k1": k_rows[:, PAIR:PACK, :],
+            "v": vT.rearrange("(p j) n -> p j n", j=PAIR),
+        }
+        packed = {}
+        for pool in ("k0", "k1", "v"):
+            packed[pool] = hold.tile([P, PAIR * T], BF16, name="packed_" + pool)
+
+        raw, got, turned, column = {}, {}, {}, {}
+        grouped, codes, scales, banks, weights, gate = {}, {}, {}, {}, {}, {}
+
+        def zero_tokens(kind, b):
             nc.vector.memset(tokens[kind][:, b * SEG : (b + 1) * SEG], 0.0)
 
-        def load_row(kind, b):
-            s = slice(b * SEG, (b + 1) * SEG)
-            nc.sync.dma_start(tokens[kind][0:1, s], source[kind][0:1, s])
+        def load_tokens(kind, b):
+            segment = slice(b * SEG, (b + 1) * SEG)
+            nc.sync.dma_start(tokens[kind][0:1, segment], token_rows[kind][0:1, segment])
 
-        def load(key, b, h):
-            start = b * SEG + h * HALF
-            t = hold.tile([P, 2, HALF], F32, name="raw_%s_%d_%d" % (key, b, h))
-            nc.sync.dma_start(t[:], pools[key][:, :, start : start + HALF])
-            raw[(key, b, h)] = t
+        def load_pairs(pool, b, half):
+            start = b * SEG + half * HALF
+            name = "raw_%s_%d_%d" % (pool, b, half)
+            t = hold.tile([P, PAIR, HALF], F32, name=name, tag=name, align_bytes=64)
+            nc.sync.dma_start(t[:], pair_rows[pool][:, :, start : start + HALF])
+            raw[(pool, b, half)] = t
 
-        for key in ("k0", "k1", "v"):
-            packed[key] = hold.tile([P, 2 * T], BF16, name="packed_" + key)
-
-        def pack(engine, key, b, h):
-            start = b * SEG + h * HALF
-            dst = packed[key][:, 2 * start : 2 * (start + HALF)].rearrange("p (n j) -> p n j", j=2)
-            src = raw[(key, b, h)][:].rearrange("p j n -> p n j")
-            if engine == "S":
-                nc.scalar.activation(dst, src, ACT.Copy)
+        def pack(engine, pool, b, half):
+            start = b * SEG + half * HALF
+            pairs = packed[pool][:, PAIR * start : PAIR * (start + HALF)].rearrange("p (n j) -> p n j", j=PAIR)
+            rows = raw[(pool, b, half)][:].rearrange("p j n -> p n j")
+            if engine == "scalar":
+                nc.scalar.activation(pairs, rows, ACT.Copy)
             else:
-                nc.vector.tensor_copy(dst, src)
+                nc.vector.tensor_copy(pairs, rows)
 
-        def gather_words(dst, key, b):
-            words = packed[key][:].bitcast(U32)
-            nc.vector.tensor_copy(dst, words[:, 0 : (b + 1) * SEG].indirect(listed(b)))
+        def gather_words(words, pool, b):
+            window = packed[pool][:].bitcast(U32)
+            nc.vector.tensor_copy(words, window[:, 0 : (b + 1) * SEG].indirect(listed(b)))
 
-        def gather_row(kind, b):
+        def gather_tokens(kind, b):
             row = hold.tile([P, N], F32, name="row_%s_%d" % (kind, b))
             nc.vector.tensor_copy(row[:], tokens[kind][:, 0 : (b + 1) * SEG].indirect(listed(b)))
-            got[(kind, b)] = row
-
-        def turn_row(kind, b):
-            turned = psum.tile([P, PACK, P], F32, name="turned_%s_%d" % (kind, b), tag="turned")
+            bank = psum.tile([P, PACK, P], F32, name="turned_%s_%d" % (kind, b), tag="turned")
             for t in range(PACK):
-                nc.tensor.transpose(turned[:, t, :], got[(kind, b)][:, t:N:PACK], ident[:])
-            banks[(kind, b)] = turned
+                nc.tensor.transpose(bank[:, t, :], row[:, t:N:PACK], ident[:])
+            turned[(kind, b)] = bank
 
-        def column(kind, b):
-            col = hold.tile([P, PACK, 1], F32, name="col_%s_%d" % (kind, b))
-            nc.vector.tensor_copy(col[:], banks[(kind, b)][:, :, 0:1])
-            cols[(kind, b)] = col
-
-        def gather_keys(b, u):
-            if u == 0:
-                got[("k", b)] = hold.tile([P, 2, 2 * N], BF16, name="k_got_%d" % b)
-            gather_words(got[("k", b)][:, u, :].bitcast(U32), "k%d" % u, b)
-
-        def group_keys(engine, b):
-            t4 = hold.tile([P, PACK * N], BF16, name="k_grouped_%d" % b, align_bytes=64)
-            copy = nc.scalar.copy if engine == "S" else nc.vector.tensor_copy
-            copy(
-                t4[:].bitcast(F32).rearrange("p (t m u) -> p m t u", t=PACK, u=2),
-                got[("k", b)][:].bitcast(F32).rearrange("p u (m t) -> p m t u", t=PACK),
-            )
-            grouped[("k", b)] = t4
+        def keep_column(kind, b):
+            t = hold.tile([P, PACK, 1], F32, name="col_%s_%d" % (kind, b))
+            nc.vector.tensor_copy(t[:], turned[(kind, b)][:, :, 0:1])
+            column[(kind, b)] = t
 
         def quantize(what, b, width):
             c = hold.tile([P, width], U32, name="codes_%s_%d" % (what, b), align_bytes=64)
@@ -109,22 +100,52 @@ def tile_attend_hstu_seg_kernel(tc, qT, kT, vT, vs, kb, og, offs, out):
             nc.vector.quantize_mx(out=c[:].bitcast(FP8X4), scales=s[:], in_=grouped[(what, b)][:])
             codes[(what, b)], scales[(what, b)] = c, s
 
+        def gather_keys(b, u):
+            if u == 0:
+                got[("k", b)] = hold.tile([P, PAIR, PAIR * N], BF16, name="k_got_%d" % b)
+            gather_words(got[("k", b)][:, u, :].bitcast(U32), "k%d" % u, b)
+
+        def group_keys(b):
+            g = hold.tile([P, PACK * N], BF16, name="k_grouped_%d" % b, align_bytes=64)
+            nc.vector.tensor_copy(
+                g[:].bitcast(F32).rearrange("p (t m u) -> p m t u", t=PACK, u=PAIR),
+                got[("k", b)][:].bitcast(F32).rearrange("p u (m t) -> p m t u", t=PACK),
+            )
+            grouped[("k", b)] = g
+
         def group_queries():
-            t4 = hold.tile([P, B * NQ * PACK], BF16, name="q_grouped", align_bytes=64)
-            view = t4[:].rearrange("p (b q j) -> p b q j", b=B, j=PACK)
+            g = hold.tile([P, B * NQ * PACK], BF16, name="q_grouped", align_bytes=64)
+            view = g[:].rearrange("p (b q j) -> p b q j", b=B, j=PACK)
             for b in range(B):
                 nc.gpsimd.tensor_scalar(
                     view[:, b, :, :], q_raw[:, b, :, :].rearrange("p j q -> p q j"), 1.0, 0.0, ALU.mult, ALU.add
                 )
-            grouped[("q", 0)] = t4
+            grouped[("q", 0)] = g
 
-        def mx(bank, left, lc, right, rc):
+        def gather_values(b):
+            g = hold.tile([P, PAIR * N], BF16, name="v_got_%d" % b)
+            gather_words(g[:].bitcast(U32), "v", b)
+            bank = psum.tile([P, PACK, P], F32, name="v_turned_%d" % b, tag="v_turned")
+            words = g[:].bitcast(F32)
+            for t in range(PACK):
+                nc.tensor.transpose(bank[:, t, :], words[:, t:N:PACK], ident[:])
+            turned[("v", b)] = bank
+
+        def group_values(b):
+            tag = ("raw_v_1_1", "v_grouped_1")[b]
+            g = hold.tile([P, DV * PACK], BF16, name="v_grouped_%d" % b, tag=tag, align_bytes=64)
+            nc.scalar.copy(
+                g[:].rearrange("p (e t) -> p e t", t=PACK), turned[("v", b)][:].bitcast(BF16).rearrange("p t e -> p e t")
+            )
+            grouped[("v", b)] = g
+
+        def multiply(bank, left, left_cols, right, right_cols):
             nc.tensor.matmul_mx(
                 out=bank,
-                lhsT=codes[left][:, lc].bitcast(FP8X4),
-                lhsT_scale=scales[left][:, lc],
-                rhs=codes[right][:, rc].bitcast(FP8X4),
-                rhs_scale=scales[right][:, rc],
+                lhsT=codes[left][:, left_cols].bitcast(FP8X4),
+                lhsT_scale=scales[left][:, left_cols],
+                rhs=codes[right][:, right_cols].bitcast(FP8X4),
+                rhs_scale=scales[right][:, right_cols],
                 start=True,
                 stop=True,
             )
@@ -132,140 +153,124 @@ def tile_attend_hstu_seg_kernel(tc, qT, kT, vT, vs, kb, og, offs, out):
         def score(b):
             bank = psum.tile([P, PACK, NQ], F32, name="score_%d" % b, tag="score")
             for t in range(PACK):
-                mx(bank[:, t, :], ("k", b), slice(t * P, (t + 1) * P), ("q", 0), slice(b * NQ, (b + 1) * NQ))
-            banks[("s", b)] = bank
+                multiply(bank[:, t, :], ("k", b), slice(t * P, (t + 1) * P), ("q", 0), slice(b * NQ, (b + 1) * NQ))
+            banks[("score", b)] = bank
 
         def silu(b):
-            p = hold.tile([P, PACK, NQ], F32, name="p_%d" % b)
+            tag = ("raw_k1_1_1", "raw_v_1_0")[b]
+            p = hold.tile([P, PACK, NQ], F32, name="p_%d" % b, tag=tag, align_bytes=64)
             for t in range(PACK):
-                nc.scalar.activation(p[:, t, :], banks[("s", b)][:, t, :], ACT.Silu, bias=cols[("kb", b)][:, t, :])
+                bias = column[("kb", b)][:, t, :]
+                nc.scalar.activation(p[:, t, :], banks[("score", b)][:, t, :], ACT.Silu, bias=bias)
             weights[b] = p
 
-        def weigh(engine, b):
-            t4 = hold.tile([P, NQ * PACK], BF16, name="w_%d" % b, align_bytes=64)
-            view = t4[:].rearrange("p (q t) -> p q t", t=PACK)
-            scale = cols[("vs", b)][:].rearrange("p t o -> p o t")
-            multiply = nc.gpsimd.tensor_tensor if engine == "G" else nc.vector.tensor_tensor
-            multiply(view, weights[b][:].rearrange("p t q -> p q t"), scale.to_broadcast([P, NQ, PACK]), ALU.mult)
-            grouped[("w", b)] = t4
-
-        def gather_values(b):
-            got[("v", b)] = hold.tile([P, 2 * N], BF16, name="v_got_%d" % b)
-            gather_words(got[("v", b)][:].bitcast(U32), "v", b)
-
-        def turn_values(b):
-            turned = psum.tile([P, PACK, P], F32, name="v_turned_%d" % b, tag="v_turned")
-            words = got[("v", b)][:].bitcast(F32)
-            for t in range(PACK):
-                nc.tensor.transpose(turned[:, t, :], words[:, t:N:PACK], ident[:])
-            banks[("v", b)] = turned
-
-        def group_values(b):
-            t4 = hold.tile([P, DV * PACK], BF16, name="v_grouped_%d" % b, align_bytes=64)
-            nc.scalar.copy(
-                t4[:].rearrange("p (e t) -> p e t", t=PACK), banks[("v", b)][:].bitcast(BF16).rearrange("p t e -> p e t")
+        def weigh(b):
+            g = hold.tile([P, NQ * PACK], BF16, name="w_%d" % b, align_bytes=64)
+            scale = column[("vs", b)][:].rearrange("p t o -> p o t")
+            nc.vector.tensor_tensor(
+                g[:].rearrange("p (q t) -> p q t", t=PACK),
+                weights[b][:].rearrange("p t q -> p q t"),
+                scale.to_broadcast([P, NQ, PACK]),
+                ALU.mult,
             )
-            grouped[("v", b)] = t4
+            grouped[("w", b)] = g
 
         def gates():
-            th = hold.tile([P, B, DV], F32, name="th")
+            th = hold.tile([P, B, DV], F32, name="th", tag="raw_v_0_1", align_bytes=64)
             nc.scalar.activation(th[:], og_raw[:], ACT.Tanh, scale=0.5)
             gate[0] = hold.tile([P, B, DV], F32, name="gate")
             nc.gpsimd.tensor_scalar(gate[0][:], th[:], 0.03125, 0.03125, ALU.mult, ALU.add)
 
         def product(b):
             y = psum.tile([P, DV], F32, name="y_%d" % b, tag="y")
-            mx(y[:], ("w", b), slice(0, NQ), ("v", b), slice(0, DV))
+            multiply(y[:], ("w", b), slice(0, NQ), ("v", b), slice(0, DV))
             banks[("y", b)] = y
 
-        def store(b):
+        def finish(b):
             res = hold.tile([P, DV], F32, name="res_%d" % b)
             nc.vector.tensor_tensor(res[:], banks[("y", b)][:], gate[0][:, b, :], ALU.mult)
             nc.sync.dma_start(out[b], res[:])
 
         q_raw = hold.tile([P, B, PACK, NQ], F32, name="q_raw")
         og_raw = hold.tile([P, B, DV], F32, name="og_raw")
+
         warm = hold.tile([P, 8], F32, name="warm")
         warmed = hold.tile([P, 8], F32, name="warmed")
         nc.gpsimd.memset(warm[:], 0.0)
         nc.scalar.activation(warmed[:], warm[:], ACT.Silu)
         ident = hold.tile([P, P], F32, name="ident")
         make_identity(nc, ident[:])
-        zero("kb", 0)
-        zero("vs", 0)
-        zero("kb", 1)
-        zero("vs", 1)
-        load("k0", 0, 0)
-        load_row("kb", 0)
-        load_row("vs", 0)
-        load("k0", 0, 1)
-        load("k1", 0, 0)
-        load_row("kb", 1)
-        load_row("vs", 1)
-        load("k1", 0, 1)
-        load("k0", 1, 0)
-        load("k0", 1, 1)
-        nc.sync.dma_start(q_raw[:], qT.rearrange("b (p j) q -> p b j q", j=PACK))
-        load("k1", 1, 0)
-        load("k1", 1, 1)
-        load("v", 0, 0)
-        load("v", 0, 1)
-        nc.sync.dma_start(og_raw[:], og.rearrange("b q e -> q b e"))
-        load("v", 1, 0)
-        load("v", 1, 1)
 
-        pack("S", "k0", 0, 0)
-        gather_row("kb", 0)
-        turn_row("kb", 0)
-        pack("S", "k0", 0, 1)
-        gather_row("vs", 0)
-        turn_row("vs", 0)
-        pack("S", "k1", 0, 0)
+        for b in range(B):
+            for kind in ("kb", "vs"):
+                zero_tokens(kind, b)
+        load_pairs("k0", 0, 0)
+        load_tokens("kb", 0)
+        load_tokens("vs", 0)
+        load_pairs("k0", 0, 1)
+        load_pairs("k1", 0, 0)
+        load_tokens("kb", 1)
+        load_tokens("vs", 1)
+        load_pairs("k1", 0, 1)
+        load_pairs("k0", 1, 0)
+        load_pairs("k0", 1, 1)
+        nc.sync.dma_start(q_raw[:], qT.rearrange("b (p j) q -> p b j q", j=PACK))
+        load_pairs("k1", 1, 0)
+        load_pairs("k1", 1, 1)
+        load_pairs("v", 0, 0)
+        load_pairs("v", 0, 1)
+        nc.sync.dma_start(og_raw[:], og.rearrange("b q e -> q b e"))
+        load_pairs("v", 1, 0)
+        load_pairs("v", 1, 1)
+
+        pack("scalar", "k0", 0, 0)
+        gather_tokens("kb", 0)
+        pack("scalar", "k0", 0, 1)
+        gather_tokens("vs", 0)
+        pack("scalar", "k1", 0, 0)
         gather_keys(0, 0)
-        column("kb", 0)
-        pack("S", "k1", 0, 1)
-        column("vs", 0)
-        gather_row("kb", 1)
-        turn_row("kb", 1)
+        keep_column("kb", 0)
+        pack("scalar", "k1", 0, 1)
+        keep_column("vs", 0)
+        gather_tokens("kb", 1)
         gather_keys(0, 1)
-        pack("S", "k0", 1, 0)
-        gather_row("vs", 1)
-        turn_row("vs", 1)
-        pack("S", "k0", 1, 1)
-        column("kb", 1)
-        group_keys("V", 0)
+        pack("scalar", "k0", 1, 0)
+        gather_tokens("vs", 1)
+        pack("scalar", "k0", 1, 1)
+        keep_column("kb", 1)
+        group_keys(0)
         group_queries()
         gather_keys(1, 0)
-        column("vs", 1)
-        pack("S", "k1", 1, 0)
+        keep_column("vs", 1)
+        pack("scalar", "k1", 1, 0)
+
         quantize("k", 0, N)
         quantize("q", 0, B * NQ)
         score(0)
-        pack("S", "k1", 1, 1)
+        pack("scalar", "k1", 1, 1)
         gather_keys(1, 1)
-        pack("S", "v", 0, 0)
+        pack("scalar", "v", 0, 0)
         silu(0)
-        group_keys("V", 1)
-        pack("S", "v", 0, 1)
+        group_keys(1)
+        pack("scalar", "v", 0, 1)
         gates()
         quantize("k", 1, N)
         score(1)
+
         gather_values(0)
-        turn_values(0)
         silu(1)
-        pack("S", "v", 1, 0)
-        pack("V", "v", 1, 1)
-        weigh("V", 0)
+        pack("scalar", "v", 1, 0)
+        pack("vector", "v", 1, 1)
+        weigh(0)
         quantize("w", 0, NQ)
         group_values(0)
         gather_values(1)
-        turn_values(1)
-        weigh("V", 1)
+        weigh(1)
         quantize("v", 0, DV)
         product(0)
         quantize("w", 1, NQ)
         group_values(1)
-        store(0)
+        finish(0)
         quantize("v", 1, DV)
         product(1)
-        store(1)
+        finish(1)

from contextlib import ExitStack

import concourse.mybir as mybir
from concourse.masks import make_identity

B, N, T, D, DV, NQ = 2, 512, 2048, 512, 256, 128
P = 128
PACK = 4
PAIR = 2
SEG = T // B
HALF = SEG // 2
LIST = N // 16

FLOPS = 2 * B * N * NQ * (D + DV)
BYTES = 4 * (B * D * NQ + D * T + DV * T + 2 * T + 2 * B * NQ * DV) + 2 * B * N

F32 = mybir.dt.float32
BF16 = mybir.dt.bfloat16
U32 = mybir.dt.uint32
U16 = mybir.dt.uint16
U8 = mybir.dt.uint8
FP8X4 = mybir.dt.float8_e4m3fn_x4
ACT = mybir.ActivationFunctionType
ALU = mybir.AluOpType


def tile_attend_hstu_seg_kernel(tc, qT, kT, vT, vs, kb, og, offs, out):
    nc = tc.nc
    with ExitStack() as ctx:
        hold = ctx.enter_context(tc.tile_pool(name="hold", bufs=1))
        psum = ctx.enter_context(tc.psum_pool(name="psum", bufs=2))

        offsets = hold.tile([P, B * LIST], U16, name="offsets")
        nc.sync.dma_start(offsets[:], offs)

        def listed(b):
            return offsets[:, b * LIST : (b + 1) * LIST]

        tokens = {}
        for kind in ("kb", "vs"):
            tokens[kind] = hold.tile([P, T], F32, name="%s_pool" % kind)
        token_rows = {"kb": kb, "vs": vs}

        k_rows = kT.rearrange("(p j) n -> p j n", j=PACK)
        pair_rows = {
            "k0": k_rows[:, 0:PAIR, :],
            "k1": k_rows[:, PAIR:PACK, :],
            "v": vT.rearrange("(p j) n -> p j n", j=PAIR),
        }
        packed = {}
        for pool in ("k0", "k1", "v"):
            packed[pool] = hold.tile([P, PAIR * T], BF16, name="packed_" + pool)

        raw, got, turned, column = {}, {}, {}, {}
        grouped, codes, scales, banks, weights, gate = {}, {}, {}, {}, {}, {}

        def zero_tokens(kind, b):
            nc.vector.memset(tokens[kind][:, b * SEG : (b + 1) * SEG], 0.0)

        def load_tokens(kind, b):
            segment = slice(b * SEG, (b + 1) * SEG)
            nc.sync.dma_start(tokens[kind][0:1, segment], token_rows[kind][0:1, segment])

        def load_pairs(pool, b, half):
            start = b * SEG + half * HALF
            name = "raw_%s_%d_%d" % (pool, b, half)
            t = hold.tile([P, PAIR, HALF], F32, name=name, tag=name, align_bytes=64)
            nc.sync.dma_start(t[:], pair_rows[pool][:, :, start : start + HALF])
            raw[(pool, b, half)] = t

        def pack(engine, pool, b, half):
            start = b * SEG + half * HALF
            pairs = packed[pool][:, PAIR * start : PAIR * (start + HALF)].rearrange("p (n j) -> p n j", j=PAIR)
            rows = raw[(pool, b, half)][:].rearrange("p j n -> p n j")
            if engine == "scalar":
                nc.scalar.activation(pairs, rows, ACT.Copy)
            else:
                nc.vector.tensor_copy(pairs, rows)

        def gather_words(words, pool, b):
            window = packed[pool][:].bitcast(U32)
            nc.vector.tensor_copy(words, window[:, 0 : (b + 1) * SEG].indirect(listed(b)))

        def gather_tokens(kind, b):
            row = hold.tile([P, N], F32, name="row_%s_%d" % (kind, b))
            nc.vector.tensor_copy(row[:], tokens[kind][:, 0 : (b + 1) * SEG].indirect(listed(b)))
            bank = psum.tile([P, PACK, P], F32, name="turned_%s_%d" % (kind, b), tag="turned")
            for t in range(PACK):
                nc.tensor.transpose(bank[:, t, :], row[:, t:N:PACK], ident[:])
            turned[(kind, b)] = bank

        def keep_column(kind, b):
            t = hold.tile([P, PACK, 1], F32, name="col_%s_%d" % (kind, b))
            nc.vector.tensor_copy(t[:], turned[(kind, b)][:, :, 0:1])
            column[(kind, b)] = t

        def quantize(what, b, width):
            c = hold.tile([P, width], U32, name="codes_%s_%d" % (what, b), align_bytes=64)
            s = hold.tile([P, width], U8, name="scales_%s_%d" % (what, b), align_bytes=64)
            nc.vector.quantize_mx(out=c[:].bitcast(FP8X4), scales=s[:], in_=grouped[(what, b)][:])
            codes[(what, b)], scales[(what, b)] = c, s

        def gather_keys(b, u):
            if u == 0:
                got[("k", b)] = hold.tile([P, PAIR, PAIR * N], BF16, name="k_got_%d" % b)
            gather_words(got[("k", b)][:, u, :].bitcast(U32), "k%d" % u, b)

        def group_keys(b):
            g = hold.tile([P, PACK * N], BF16, name="k_grouped_%d" % b, align_bytes=64)
            nc.vector.tensor_copy(
                g[:].bitcast(F32).rearrange("p (t m u) -> p m t u", t=PACK, u=PAIR),
                got[("k", b)][:].bitcast(F32).rearrange("p u (m t) -> p m t u", t=PACK),
            )
            grouped[("k", b)] = g

        def group_queries():
            g = hold.tile([P, B * NQ * PACK], BF16, name="q_grouped", align_bytes=64)
            view = g[:].rearrange("p (b q j) -> p b q j", b=B, j=PACK)
            for b in range(B):
                nc.gpsimd.tensor_scalar(
                    view[:, b, :, :], q_raw[:, b, :, :].rearrange("p j q -> p q j"), 1.0, 0.0, ALU.mult, ALU.add
                )
            grouped[("q", 0)] = g

        def gather_values(b):
            g = hold.tile([P, PAIR * N], BF16, name="v_got_%d" % b)
            gather_words(g[:].bitcast(U32), "v", b)
            bank = psum.tile([P, PACK, P], F32, name="v_turned_%d" % b, tag="v_turned")
            words = g[:].bitcast(F32)
            for t in range(PACK):
                nc.tensor.transpose(bank[:, t, :], words[:, t:N:PACK], ident[:])
            turned[("v", b)] = bank

        def group_values(b):
            tag = ("raw_v_1_1", "v_grouped_1")[b]
            g = hold.tile([P, DV * PACK], BF16, name="v_grouped_%d" % b, tag=tag, align_bytes=64)
            nc.scalar.copy(
                g[:].rearrange("p (e t) -> p e t", t=PACK), turned[("v", b)][:].bitcast(BF16).rearrange("p t e -> p e t")
            )
            grouped[("v", b)] = g

        def multiply(bank, left, left_cols, right, right_cols):
            nc.tensor.matmul_mx(
                out=bank,
                lhsT=codes[left][:, left_cols].bitcast(FP8X4),
                lhsT_scale=scales[left][:, left_cols],
                rhs=codes[right][:, right_cols].bitcast(FP8X4),
                rhs_scale=scales[right][:, right_cols],
                start=True,
                stop=True,
            )

        def score(b):
            bank = psum.tile([P, PACK, NQ], F32, name="score_%d" % b, tag="score")
            for t in range(PACK):
                multiply(bank[:, t, :], ("k", b), slice(t * P, (t + 1) * P), ("q", 0), slice(b * NQ, (b + 1) * NQ))
            banks[("score", b)] = bank

        def silu(b):
            tag = ("raw_k1_1_1", "raw_v_1_0")[b]
            p = hold.tile([P, PACK, NQ], F32, name="p_%d" % b, tag=tag, align_bytes=64)
            for t in range(PACK):
                bias = column[("kb", b)][:, t, :]
                nc.scalar.activation(p[:, t, :], banks[("score", b)][:, t, :], ACT.Silu, bias=bias)
            weights[b] = p

        def weigh(b):
            g = hold.tile([P, NQ * PACK], BF16, name="w_%d" % b, align_bytes=64)
            scale = column[("vs", b)][:].rearrange("p t o -> p o t")
            nc.vector.tensor_tensor(
                g[:].rearrange("p (q t) -> p q t", t=PACK),
                weights[b][:].rearrange("p t q -> p q t"),
                scale.to_broadcast([P, NQ, PACK]),
                ALU.mult,
            )
            grouped[("w", b)] = g

        def gates():
            th = hold.tile([P, B, DV], F32, name="th", tag="raw_v_0_1", align_bytes=64)
            nc.scalar.activation(th[:], og_raw[:], ACT.Tanh, scale=0.5)
            gate[0] = hold.tile([P, B, DV], F32, name="gate")
            nc.gpsimd.tensor_scalar(gate[0][:], th[:], 0.03125, 0.03125, ALU.mult, ALU.add)

        def product(b):
            y = psum.tile([P, DV], F32, name="y_%d" % b, tag="y")
            multiply(y[:], ("w", b), slice(0, NQ), ("v", b), slice(0, DV))
            banks[("y", b)] = y

        def finish(b):
            res = hold.tile([P, DV], F32, name="res_%d" % b)
            nc.vector.tensor_tensor(res[:], banks[("y", b)][:], gate[0][:, b, :], ALU.mult)
            nc.sync.dma_start(out[b], res[:])

        q_raw = hold.tile([P, B, PACK, NQ], F32, name="q_raw")
        og_raw = hold.tile([P, B, DV], F32, name="og_raw")

        warm = hold.tile([P, 8], F32, name="warm")
        warmed = hold.tile([P, 8], F32, name="warmed")
        nc.gpsimd.memset(warm[:], 0.0)
        nc.scalar.activation(warmed[:], warm[:], ACT.Silu)
        ident = hold.tile([P, P], F32, name="ident")
        make_identity(nc, ident[:])

        for b in range(B):
            for kind in ("kb", "vs"):
                zero_tokens(kind, b)
        load_pairs("k0", 0, 0)
        load_tokens("kb", 0)
        load_tokens("vs", 0)
        load_pairs("k0", 0, 1)
        load_pairs("k1", 0, 0)
        load_tokens("kb", 1)
        load_tokens("vs", 1)
        load_pairs("k1", 0, 1)
        load_pairs("k0", 1, 0)
        load_pairs("k0", 1, 1)
        nc.sync.dma_start(q_raw[:], qT.rearrange("b (p j) q -> p b j q", j=PACK))
        load_pairs("k1", 1, 0)
        load_pairs("k1", 1, 1)
        load_pairs("v", 0, 0)
        load_pairs("v", 0, 1)
        nc.sync.dma_start(og_raw[:], og.rearrange("b q e -> q b e"))
        load_pairs("v", 1, 0)
        load_pairs("v", 1, 1)

        pack("scalar", "k0", 0, 0)
        gather_tokens("kb", 0)
        pack("scalar", "k0", 0, 1)
        gather_tokens("vs", 0)
        pack("scalar", "k1", 0, 0)
        gather_keys(0, 0)
        keep_column("kb", 0)
        pack("scalar", "k1", 0, 1)
        keep_column("vs", 0)
        gather_tokens("kb", 1)
        gather_keys(0, 1)
        pack("scalar", "k0", 1, 0)
        gather_tokens("vs", 1)
        pack("scalar", "k0", 1, 1)
        keep_column("kb", 1)
        group_keys(0)
        group_queries()
        gather_keys(1, 0)
        keep_column("vs", 1)
        pack("scalar", "k1", 1, 0)

        quantize("k", 0, N)
        quantize("q", 0, B * NQ)
        score(0)
        pack("scalar", "k1", 1, 1)
        gather_keys(1, 1)
        pack("scalar", "v", 0, 0)
        silu(0)
        group_keys(1)
        pack("scalar", "v", 0, 1)
        gates()
        quantize("k", 1, N)
        score(1)

        gather_values(0)
        silu(1)
        pack("scalar", "v", 1, 0)
        pack("vector", "v", 1, 1)
        weigh(0)
        quantize("w", 0, NQ)
        group_values(0)
        gather_values(1)
        weigh(1)
        quantize("v", 0, DV)
        product(0)
        quantize("w", 1, NQ)
        group_values(1)
        finish(0)
        quantize("v", 1, DV)
        product(1)
        finish(1)
